import numpy as np
import ml_dtypes


def mxq(x, axis, fmt="e4m3"):
    dtype, down = {"e4m3": (ml_dtypes.float8_e4m3fn, 7), "e5m2": (ml_dtypes.float8_e5m2, 14)}[fmt]
    v = np.moveaxis(np.asarray(x, np.float32).astype(ml_dtypes.bfloat16).astype(np.float64), axis, -1)
    blocks = v.reshape(v.shape[:-1] + (-1, 32))
    amax = np.abs(blocks).max(-1, keepdims=True)
    byte = np.maximum(np.where(amax > 0, np.frexp(amax)[1] - 1 + 127, 0) - down, 1)
    scale = np.exp2(byte - 127.0)
    codes = (blocks / scale).astype(np.float32).astype(dtype).astype(np.float64)
    return np.moveaxis((codes * scale).reshape(v.shape), -1, axis)


WIDE = False


def mx_kscale(k):
    if not WIDE:
        return np.ones(k)
    levels = np.array([10, -10, 5, -5, 0])
    if k % 512:
        return np.exp2(np.random.permutation(np.resize(levels, k // 32))).repeat(32)
    a = np.empty((k // 512, 16))
    for p in range(k // 512):
        a[p, :8] = np.random.permutation(np.resize(levels, 8))
        for g in range(8):
            far = levels[np.abs(levels - a[p, g]) >= 10]
            a[p, g + 8] = far[np.random.randint(len(far))]
    return np.exp2(a.ravel()).repeat(32)


BF16 = ml_dtypes.bfloat16


def bf(x):
    return np.asarray(x, np.float32).astype(BF16)


def f64(x):
    return np.asarray(x).astype(np.float64)


E2M1 = np.array([0.0, 0.5, 1.0, 1.5, 2.0, 3.0, 4.0, 6.0, -0.0, -0.5, -1.0, -1.5, -2.0, -3.0, -4.0, -6.0])


def pack_weight(w, fmt):
    k, n = w.shape
    w = f64(bf(w)).reshape(k // 32, 32, n)
    amax = np.abs(w).max(1)
    if fmt == "e4m3":
        byte = np.frexp(amax)[1] - 1 + 127 - 7
    else:
        mant, ex = np.frexp(amax / 6.0)
        byte = np.where(mant > 0.5, ex, ex - 1) + 127
    byte = np.clip(np.where(amax > 0, byte, 1), 1, 254)
    scaled = (w * np.exp2(127.0 - byte)[:, None, :]).reshape(k, n).astype(np.float32)
    by_word = np.ascontiguousarray(scaled.reshape(k // 512, 128, 4, n).transpose(0, 1, 3, 2))
    if fmt == "e4m3":
        words = by_word.astype(ml_dtypes.float8_e4m3fn).view(np.uint8)
    else:
        c = by_word.astype(ml_dtypes.float4_e2m1fn).view(np.uint8) & 0xF
        words = c[..., 0::2] | (c[..., 1::2] << 4)
    return np.ascontiguousarray(words), np.ascontiguousarray(byte.astype(np.uint8).reshape(k // 512, 16, n))


def unpack_weight(words, scales, fmt):
    g, p, n, _ = words.shape
    if fmt == "e4m3":
        vals = np.ascontiguousarray(words).view(ml_dtypes.float8_e4m3fn).astype(np.float64)
    else:
        nib = np.empty((g, p, n, 4), np.uint8)
        nib[..., 0::2] = words & 0xF
        nib[..., 1::2] = words >> 4
        vals = E2M1[nib]
    vals = vals * np.repeat(np.exp2(scales.astype(np.float64) - 127.0), 8, axis=1)[..., None]
    return vals.transpose(0, 1, 3, 2).reshape(g * 512, n)
def pack4(w):
    words, scales = pack_weight(w, "e2m1")
    return words.reshape(words.shape[0], 128, -1), scales


def unpack4(words, scales):
    return unpack_weight(words.reshape(words.shape[0], 128, -1, 2), scales, "e2m1")


def planes(Y):
    n, m = Y.shape
    b = f64(bf(Y)).reshape(n // 32, 32, m)
    amax = np.abs(b).max(1)
    byte = np.clip(np.where(amax > 0, np.frexp(amax)[1] - 1 + 127 - 7, 1), 1, 254)
    codes = (b * np.exp2(127.0 - byte)[:, None, :]).reshape(n, m).astype(np.float32).astype(ml_dtypes.float8_e4m3fn).view(np.uint8)
    words = codes.reshape(n // 512, 128, 4, m).transpose(0, 1, 3, 2)
    return np.ascontiguousarray(words), np.ascontiguousarray(byte.astype(np.uint8).reshape(n // 512, 16, m))


G, R, D, E, C = 4, 1024, 1024, 512, 512
SCALE = 16.0

def setup_inputs():
    s, t = mx_kscale(D), mx_kscale(E)
    x = np.random.randn(G, R, D) * np.exp(0.3 * np.random.randn(G, R, 1))
    len_scale = SCALE / np.sqrt((x * x).sum(axis=2))
    w = np.random.randn(G, D, E) / np.sqrt(E)
    v = np.random.randn(G, E, C)
    v = v / np.sqrt((v * v).sum(axis=1, keepdims=True))
    w_words, w_scales = pack4((w * t / s[:, None]).reshape(G * D, E))
    v_words, v_scales = pack4((v / t[:, None]).reshape(G * E, C))
    margin = np.random.uniform(0.1, 0.3, (G, C))
    angle = np.random.uniform(0.3, 1.3, (G, C))
    gain = 1 + 0.1 * np.random.randn(G, C)
    return {"x": bf(x * s), "w_words": w_words, "w_scales": w_scales,
            "v_words": v_words, "v_scales": v_scales, "len_scale": bf(len_scale),
            "cos_gain": bf(gain * np.cos(margin)),
            "sine_term": bf(gain * SCALE * np.sin(margin) * np.sin(angle)),
            "shift": bf(-2.0 + 0.3 * np.random.randn(G, R))}

def reference(x, w_words, w_scales, v_words, v_scales, len_scale, cos_gain, sine_term, shift):
    w = unpack4(w_words, w_scales).reshape(G, D, E)
    v = unpack4(v_words, v_scales).reshape(G, E, C)
    h = mxq(f64(x), 2, "e4m3") @ w
    e = h * f64(len_scale)[:, :, None]
    c = mxq(e, 2, "e4m3") @ v
    y = np.exp(c * f64(cos_gain)[:, None, :] - f64(sine_term)[:, None, :] - f64(shift)[:, :, None])
    Y = y.reshape(G * R, C).T
    words, scales = planes(Y)
    return y, words, scales

@@ -1,0 +1,270 @@
+from contextlib import ExitStack
+
+import concourse.mybir as mybir
+from concourse.masks import make_identity
+
+G, R, D, E, C = 4, 1024, 1024, 512, 512
+FLOPS = 2 * G * R * (D * E + E * C)
+
+F32 = mybir.dt.float32
+BF16 = mybir.dt.bfloat16
+I32 = mybir.dt.int32
+U32 = mybir.dt.uint32
+U8 = mybir.dt.uint8
+FP8X4 = mybir.dt.float8_e4m3fn_x4
+FP4X4 = mybir.dt.float4_e2m1fn_x4
+ACT = mybir.ActivationFunctionType
+ALU = mybir.AluOpType
+
+P = 128
+K_PASS = 512
+TILES = G * R // P
+TILES_PER_DOMAIN = R // P
+X_PASSES = D // K_PASS
+X_LEAD = 4
+WORDS_GROUP = 2
+SCALE_STORES = (15, 27, 31)
+
+
+def tile_domain_margin_softmax_weights_k7_kernel(
+    tc, x, w_words, w_scales, v_words, v_scales, len_scale, cos_gain, sine_term, shift, out_0, out_1, out_2
+):
+    nc = tc.nc
+    x_rows = x.rearrange("g r d -> (g r) d")
+    y_rows = out_0.rearrange("g r c -> (g r) c")
+    w_words32 = w_words.bitcast(I32)
+    v_words32 = v_words.bitcast(I32)
+    w_scales32 = w_scales.bitcast(I32)
+    v_scales32 = v_scales.bitcast(I32)
+    y_words32 = out_1[0].rearrange("p m t -> p (m t)").bitcast(I32)
+    y_scales32 = out_2[0].bitcast(I32)
+
+    with ExitStack() as ctx:
+        keep = ctx.enter_context(tc.tile_pool(name="keep", bufs=1))
+        work = ctx.enter_context(tc.tile_pool(name="work", bufs=3))
+        psum = ctx.enter_context(tc.psum_pool(name="psum", bufs=2))
+        ctx.enter_context(tc.manual_schedule())
+
+        ident = keep.tile([P, P], F32, name="ident")
+        w_plane = keep.tile([P, G * X_PASSES, E], U8, name="w_plane", align_bytes=64)
+        v_plane = keep.tile([P, G, C], U8, name="v_plane", align_bytes=64)
+        y_plane = keep.tile([P, G * R], U8, name="y_plane", align_bytes=64)
+        row_vecs = keep.tile([P, P], BF16, name="row_vecs")
+        row_vecs32 = keep.tile([P, P], F32, name="row_vecs32")
+        row_cols = keep.tile([P, 2 * TILES], F32, name="row_cols")
+        warm = keep.tile([P, 1], F32, name="warm")
+        warm_out = keep.tile([P, 1], F32, name="warm_out")
+
+        x_sb, x_q, h_ps, e_bf, turned, e_q, c_ps, z_sb, y_sb, y_bf = ({} for i in range(10))
+        x_grouped, w_sb, v_sb, gain_sb, sine_sb, y_codes = ({} for i in range(6))
+
+        def load_x(n):
+            x_sb[n] = work.tile([P, D], BF16, name="x_sb", bufs=X_LEAD + 2)
+            nc.sync.dma_start(out=x_sb[n][:], in_=x_rows[n * P : (n + 1) * P, :])
+
+        def load_w(u):
+            w_sb[u] = work.tile([P, X_PASSES, 2 * E], U8, name="w_sb", bufs=2, align_bytes=64)
+            nc.sync.dma_start(
+                out=w_sb[u][:].bitcast(I32),
+                in_=w_words32[X_PASSES * u : X_PASSES * (u + 1)].rearrange("g p n -> p g n"),
+            )
+
+        def load_v(u):
+            v_sb[u] = work.tile([P, 2 * C], U8, name="v_sb", bufs=2, align_bytes=64)
+            nc.sync.dma_start(out=v_sb[u][:].bitcast(I32), in_=v_words32[u])
+
+        def load_speaker_rows(u):
+            gain_sb[u] = work.tile([P, C], BF16, name="gain_sb", bufs=2)
+            sine_sb[u] = work.tile([P, C], BF16, name="sine_sb", bufs=2)
+            nc.sync.dma_start(out=gain_sb[u][:], in_=cos_gain[u].partition_broadcast(P))
+            nc.sync.dma_start(out=sine_sb[u][:], in_=sine_term[u].partition_broadcast(P))
+
+        def load_plane(plane, scales32):
+            for q in range(4):
+                nc.sync.dma_start(
+                    out=plane[32 * q : 32 * q + 4].bitcast(I32),
+                    in_=scales32[:, 4 * q : 4 * q + 4, :].rearrange("g r n -> r g n"),
+                )
+
+        def live(n):
+            return 0 <= n < TILES
+
+        nc.vector.memset(w_plane[:].bitcast(I32), 0)
+        nc.vector.memset(warm[:], 0.0)
+        nc.vector.memset(row_vecs32[2 * TILES :, :], 0.0)
+        nc.vector.memset(v_plane[:].bitcast(I32), 0)
+        nc.scalar.activation(out=warm_out[:], in_=warm[:], func=ACT.Exp)
+        make_identity(nc, ident[:])
+        load_x(0)
+        load_w(0)
+        load_plane(w_plane, w_scales32)
+        load_x(1)
+        nc.sync.dma_start(out=row_vecs[:TILES, :], in_=len_scale.rearrange("g (n p) -> (g n) p", p=P))
+        nc.sync.dma_start(out=row_vecs[TILES : 2 * TILES, :], in_=shift.rearrange("g (n p) -> (g n) p", p=P))
+        load_x(2)
+        load_x(3)
+        load_v(0)
+        load_plane(v_plane, v_scales32)
+        load_speaker_rows(0)
+
+        def turn_row_vectors():
+            nc.vector.tensor_copy(out=row_vecs32[: 2 * TILES, :], in_=row_vecs[: 2 * TILES, :])
+            cols_ps = psum.tile([P, C], F32, name="c_ps")
+            nc.tensor.transpose(cols_ps[:, :P], row_vecs32[:], ident[:])
+            nc.vector.tensor_copy(out=row_cols[:], in_=cols_ps[:, : 2 * TILES])
+
+        for n in range(TILES + 9):
+            if live(n + X_LEAD):
+                load_x(n + X_LEAD)
+            u_next, phase = divmod(n, TILES_PER_DOMAIN)
+            u_next = u_next + 1
+            if u_next < G and phase == 4:
+                load_w(u_next)
+            if u_next < G and phase == 6:
+                load_v(u_next)
+            if u_next < G and phase == 7:
+                load_speaker_rows(u_next)
+            if n == 1:
+                turn_row_vectors()
+
+            n_e, n_y = n - 3, n - 7
+            if live(n_e) or live(n_y):
+                ey_ps = psum.tile([P, 2, 2, P], F32, name="ey_ps")
+                for half, src, m in ((0, e_bf, n_e), (1, y_bf, n_y)):
+                    if live(m):
+                        words = src[m][:].bitcast(F32)
+                        for u in range(2):
+                            nc.tensor.transpose(ey_ps[:, half, u, :], words[:, u * P : (u + 1) * P], ident[:])
+            if live(n):
+                xt_ps = psum.tile([P, X_PASSES, 2, P], F32, name="xt_ps")
+                words = x_sb[n][:].bitcast(F32)
+                for g in range(X_PASSES):
+                    for u in range(2):
+                        nc.tensor.transpose(
+                            xt_ps[:, g, u, :], words[:, 2 * P * g + u : 2 * P * (g + 1) : 2], ident[:]
+                        )
+
+            m = n - 2
+            if live(m):
+                e_bf[m] = work.tile([P, E], BF16, name="e_bf")
+                nc.scalar.activation(
+                    out=e_bf[m][:].rearrange("p (u m e) -> p u m e", u=2, e=2),
+                    in_=h_ps[m][:].rearrange("p (m u e) -> p u m e", u=2, e=2),
+                    func=ACT.Copy,
+                    scale=row_cols[:, m : m + 1],
+                )
+            y_half_on_vector = live(n_y) and live(n_e) and n % 2 == 0
+            if live(n_e) or live(n_y):
+                turned[n] = work.tile([P, 2, 4 * P], BF16, name="turned", align_bytes=64)
+                lo = 0 if live(n_e) else 1
+                hi = 2 if live(n_y) and not y_half_on_vector else 1
+                nc.scalar.copy(
+                    out=turned[n][:, lo:hi, :].bitcast(F32).rearrange("p h (r u) -> p h r u", u=2),
+                    in_=ey_ps[:, lo:hi].rearrange("p h u r -> p h r u"),
+                )
+            m = n - 6
+            if live(m):
+                y_sb[m] = work.tile([P, C], F32, name="y_sb", bufs=4)
+                nc.scalar.activation(out=y_sb[m][:], in_=z_sb[m][:], func=ACT.Exp)
+                nc.sync.dma_start(out=y_rows[m * P : (m + 1) * P, :], in_=y_sb[m][:])
+            if live(n):
+                x_grouped[n] = work.tile([P, D], BF16, name="x_grouped", align_bytes=64)
+                nc.scalar.copy(
+                    out=x_grouped[n][:].bitcast(F32).rearrange("p (g r u) -> p g r u", g=X_PASSES, u=2),
+                    in_=xt_ps[:].rearrange("p g u r -> p g r u"),
+                )
+
+            m = n - 5
+            if live(m):
+                scaled = work.tile([P, C], F32, name="scaled", bufs=2)
+                nc.vector.tensor_tensor(
+                    out=scaled[:], in0=c_ps[m][:], in1=gain_sb[m // TILES_PER_DOMAIN][:], op=ALU.mult
+                )
+            m = n - 1
+            if live(m):
+                codes = work.tile([P, D // 4], U32, name="x_codes", align_bytes=64)
+                plane = work.tile([P, D // 4], U8, name="x_plane", align_bytes=64)
+                nc.vector.quantize_mx(out=codes[:].bitcast(FP8X4), scales=plane[:], in_=x_grouped[m][:])
+                x_q[m] = (codes, plane)
+            m = n - 5
+            if live(m):
+                z_sb[m] = work.tile([P, C], F32, name="z_sb")
+                nc.vector.scalar_tensor_tensor(
+                    out=z_sb[m][:],
+                    in0=scaled[:],
+                    scalar=row_cols[:, TILES + m : TILES + m + 1],
+                    in1=sine_sb[m // TILES_PER_DOMAIN][:],
+                    op0=ALU.subtract,
+                    op1=ALU.subtract,
+                )
+            m = n - 4
+            if live(m):
+                codes = work.tile([P, P], U32, name="e_codes", align_bytes=64)
+                plane = work.tile([P, P], U8, name="e_plane", align_bytes=64)
+                nc.vector.quantize_mx(out=codes[:].bitcast(FP8X4), scales=plane[:], in_=turned[n - 1][:, 0, :])
+                e_q[m] = (codes, plane)
+            m = n - 8
+            if live(m):
+                group, slot = divmod(m, WORDS_GROUP)
+                if slot == 0:
+                    y_codes[group] = work.tile([P, WORDS_GROUP * P], U32, name="y_codes", align_bytes=64)
+                nc.vector.quantize_mx(
+                    out=y_codes[group][:, slot * P : (slot + 1) * P].bitcast(FP8X4),
+                    scales=y_plane[:, m * P : (m + 1) * P],
+                    in_=turned[n - 1][:, 1, :],
+                )
+                if slot == WORDS_GROUP - 1:
+                    nc.sync.dma_start(
+                        out=y_words32[:, group * WORDS_GROUP * P : (group + 1) * WORDS_GROUP * P],
+                        in_=y_codes[group][:].bitcast(I32),
+                    )
+                if m in SCALE_STORES:
+                    i = SCALE_STORES.index(m)
+                    first = 0 if i == 0 else SCALE_STORES[i - 1] + 1
+                    for q in range(4):
+                        nc.sync.dma_start(
+                            out=y_scales32[4 * q : 4 * q + 4, first * P // 4 : (m + 1) * P // 4],
+                            in_=y_plane[32 * q : 32 * q + 4, first * P : (m + 1) * P].bitcast(I32),
+                        )
+            m = n - 6
+            if live(m):
+                y_bf[m] = work.tile([P, C], BF16, name="y_bf")
+                nc.vector.tensor_copy(
+                    out=y_bf[m][:].rearrange("p (u m e) -> p u m e", u=2, e=2),
+                    in_=y_sb[m][:].rearrange("p (m u e) -> p u m e", u=2, e=2),
+                )
+            if y_half_on_vector:
+                nc.vector.tensor_copy(
+                    out=turned[n][:, 1, :].bitcast(F32).rearrange("p (r u) -> p r u", u=2),
+                    in_=ey_ps[:, 1].rearrange("p u r -> p r u"),
+                )
+
+            m = n - 1
+            if live(m):
+                u = m // TILES_PER_DOMAIN
+                h_ps[m] = psum.tile([P, E], F32, name="h_ps")
+                codes, plane = x_q[m]
+                for g in range(X_PASSES):
+                    nc.tensor.matmul_mx(
+                        out=h_ps[m][:],
+                        lhsT=codes[:, g * P : (g + 1) * P].bitcast(FP8X4),
+                        lhsT_scale=plane[:, g * P : (g + 1) * P],
+                        rhs=w_sb[u][:, g, :].bitcast(FP4X4),
+                        rhs_scale=w_plane[:, X_PASSES * u + g, :],
+                        start=(g == 0),
+                        stop=(g == X_PASSES - 1),
+                    )
+            m = n - 4
+            if live(m):
+                u = m // TILES_PER_DOMAIN
+                c_ps[m] = psum.tile([P, C], F32, name="c_ps")
+                codes, plane = e_q[m]
+                nc.tensor.matmul_mx(
+                    out=c_ps[m][:],
+                    lhsT=codes[:].bitcast(FP8X4),
+                    lhsT_scale=plane[:],
+                    rhs=v_sb[u][:].bitcast(FP4X4),
+                    rhs_scale=v_plane[:, u, :],
+                    start=True,
+                    stop=True,
+                )

@@ -21,9 +21,13 @@ K_PASS = 512
 TILES = G * R // P
 TILES_PER_DOMAIN = R // P
 X_PASSES = D // K_PASS
-X_LEAD = 4
-WORDS_GROUP = 2
-SCALE_STORES = (15, 27, 31)
+X_LEAD = 6
+PAIRS = TILES // 2
+SLICES = C // P
+SCALE_STORES = (7, 13, 15)
+PSUM_BANKS = 8
+SCALAR_LOGITS_FROM = 99
+SCALAR_GROUPS_FROM = 11
 
 
 def tile_domain_margin_softmax_weights_k7_kernel(
@@ -42,25 +46,42 @@ def tile_domain_margin_softmax_weights_k7_kernel(
     with ExitStack() as ctx:
         keep = ctx.enter_context(tc.tile_pool(name="keep", bufs=1))
         work = ctx.enter_context(tc.tile_pool(name="work", bufs=3))
-        psum = ctx.enter_context(tc.psum_pool(name="psum", bufs=2))
+        psum = ctx.enter_context(tc.psum_pool(name="psum", bufs=1))
         ctx.enter_context(tc.manual_schedule())
 
         ident = keep.tile([P, P], F32, name="ident")
         w_plane = keep.tile([P, G * X_PASSES, E], U8, name="w_plane", align_bytes=64)
         v_plane = keep.tile([P, G, C], U8, name="v_plane", align_bytes=64)
         y_plane = keep.tile([P, G * R], U8, name="y_plane", align_bytes=64)
-        row_vecs = keep.tile([P, P], BF16, name="row_vecs")
-        row_vecs32 = keep.tile([P, P], F32, name="row_vecs32")
-        row_cols = keep.tile([P, 2 * TILES], F32, name="row_cols")
+        len_rows = keep.tile([P, P], BF16, name="len_rows")
+        len_rows32 = keep.tile([P, P], F32, name="len_rows32")
+        len_cols = keep.tile([P, TILES], F32, name="len_cols")
+        late_rows = keep.tile([P, P], BF16, name="late_rows")
+        late_rows32 = keep.tile([P, P], F32, name="late_rows32")
+        neg_cols = keep.tile([P, TILES + G * SLICES], F32, name="neg_cols")
+        gain_cols = keep.tile([P, G * SLICES], F32, name="gain_cols")
         warm = keep.tile([P, 1], F32, name="warm")
         warm_out = keep.tile([P, 1], F32, name="warm_out")
 
-        x_sb, x_q, h_ps, e_bf, turned, e_q, c_ps, z_sb, y_sb, y_bf = ({} for i in range(10))
-        x_grouped, w_sb, v_sb, gain_sb, sine_sb, y_codes = ({} for i in range(6))
+        x_sb, x_ps, x_grouped, x_q, h_ps, e_bf, e_ps, e_grouped, e_q = ({} for i in range(9))
+        c_ps, z_sb, z_ps, y_sb, y_bf, y_ps, y_grouped, w_sb, v_sb = ({} for i in range(9))
+        banks_used = []
 
-        def load_x(n):
-            x_sb[n] = work.tile([P, D], BF16, name="x_sb", bufs=X_LEAD + 2)
-            nc.sync.dma_start(out=x_sb[n][:], in_=x_rows[n * P : (n + 1) * P, :])
+        def next_bank(shape):
+            bank = psum.tile(shape, F32, name="bank%d" % (len(banks_used) % PSUM_BANKS))
+            banks_used.append(bank)
+            return bank
+
+        def load_x_tile(n):
+            first = keep.tile([P, D], BF16, name="x_first%d" % n)
+            nc.sync.dma_start(out=first[:], in_=x_rows[n * P : (n + 1) * P, :])
+            x_sb[n] = first[:]
+
+        def load_x_pair(j):
+            pair = work.tile([P, 2, D], BF16, name="x_pair", bufs=4)
+            nc.sync.dma_start(out=pair[:], in_=x_rows[2 * P * j : 2 * P * (j + 1), :].rearrange("(i p) d -> p i d", p=P))
+            x_sb[2 * j] = pair[:, 0, :]
+            x_sb[2 * j + 1] = pair[:, 1, :]
 
         def load_w(u):
             w_sb[u] = work.tile([P, X_PASSES, 2 * E], U8, name="w_sb", bufs=2, align_bytes=64)
@@ -73,12 +94,6 @@ def tile_domain_margin_softmax_weights_k7_kernel(
             v_sb[u] = work.tile([P, 2 * C], U8, name="v_sb", bufs=2, align_bytes=64)
             nc.sync.dma_start(out=v_sb[u][:].bitcast(I32), in_=v_words32[u])
 
-        def load_speaker_rows(u):
-            gain_sb[u] = work.tile([P, C], BF16, name="gain_sb", bufs=2)
-            sine_sb[u] = work.tile([P, C], BF16, name="sine_sb", bufs=2)
-            nc.sync.dma_start(out=gain_sb[u][:], in_=cos_gain[u].partition_broadcast(P))
-            nc.sync.dma_start(out=sine_sb[u][:], in_=sine_term[u].partition_broadcast(P))
-
         def load_plane(plane, scales32):
             for q in range(4):
                 nc.sync.dma_start(
@@ -86,185 +101,236 @@ def tile_domain_margin_softmax_weights_k7_kernel(
                     in_=scales32[:, 4 * q : 4 * q + 4, :].rearrange("g r n -> r g n"),
                 )
 
-        def live(n):
-            return 0 <= n < TILES
+        def turn_len_scale():
+            nc.vector.tensor_copy(out=len_rows32[:TILES, :], in_=len_rows[:TILES, :])
+            bank = next_bank([P, P])
+            nc.tensor.transpose(bank[:], len_rows32[:], ident[:])
+            nc.vector.tensor_copy(out=len_cols[:], in_=bank[:, :TILES])
 
-        nc.vector.memset(w_plane[:].bitcast(I32), 0)
-        nc.vector.memset(warm[:], 0.0)
-        nc.vector.memset(row_vecs32[2 * TILES :, :], 0.0)
-        nc.vector.memset(v_plane[:].bitcast(I32), 0)
-        nc.scalar.activation(out=warm_out[:], in_=warm[:], func=ACT.Exp)
-        make_identity(nc, ident[:])
-        load_x(0)
-        load_w(0)
-        load_plane(w_plane, w_scales32)
-        load_x(1)
-        nc.sync.dma_start(out=row_vecs[:TILES, :], in_=len_scale.rearrange("g (n p) -> (g n) p", p=P))
-        nc.sync.dma_start(out=row_vecs[TILES : 2 * TILES, :], in_=shift.rearrange("g (n p) -> (g n) p", p=P))
-        load_x(2)
-        load_x(3)
-        load_v(0)
-        load_plane(v_plane, v_scales32)
-        load_speaker_rows(0)
+        def turn_late_vectors():
+            nc.vector.tensor_copy(out=late_rows32[: 2 * TILES, :], in_=late_rows[: 2 * TILES, :])
+            bank = next_bank([P, P])
+            nc.tensor.transpose(bank[:], late_rows32[:], ident[:])
+            nc.vector.tensor_scalar(
+                out=neg_cols[:], in0=bank[:, : TILES + G * SLICES], scalar1=-1.0, scalar2=None, op0=ALU.mult
+            )
+            nc.vector.tensor_copy(out=gain_cols[:], in_=bank[:, TILES + G * SLICES : 2 * TILES])
 
-        def turn_row_vectors():
-            nc.vector.tensor_copy(out=row_vecs32[: 2 * TILES, :], in_=row_vecs[: 2 * TILES, :])
-            cols_ps = psum.tile([P, C], F32, name="c_ps")
-            nc.tensor.transpose(cols_ps[:, :P], row_vecs32[:], ident[:])
-            nc.vector.tensor_copy(out=row_cols[:], in_=cols_ps[:, : 2 * TILES])
+        def turn_x(n):
+            x_ps[n] = next_bank([P, X_PASSES, 2, P])
+            words = x_sb[n].bitcast(F32)
+            for g in range(X_PASSES):
+                for u in range(2):
+                    nc.tensor.transpose(x_ps[n][:, g, u, :], words[:, 2 * P * g + u : 2 * P * (g + 1) : 2], ident[:])
 
-        for n in range(TILES + 9):
-            if live(n + X_LEAD):
-                load_x(n + X_LEAD)
-            u_next, phase = divmod(n, TILES_PER_DOMAIN)
-            u_next = u_next + 1
-            if u_next < G and phase == 4:
-                load_w(u_next)
-            if u_next < G and phase == 6:
-                load_v(u_next)
-            if u_next < G and phase == 7:
-                load_speaker_rows(u_next)
-            if n == 1:
-                turn_row_vectors()
+        def group_x(n):
+            x_grouped[n] = work.tile([P, D], BF16, name="x_grouped", align_bytes=64)
+            nc.scalar.copy(
+                out=x_grouped[n][:].bitcast(F32).rearrange("p (g r u) -> p g r u", g=X_PASSES, u=2),
+                in_=x_ps[n][:].rearrange("p g u r -> p g r u"),
+            )
 
-            n_e, n_y = n - 3, n - 7
-            if live(n_e) or live(n_y):
-                ey_ps = psum.tile([P, 2, 2, P], F32, name="ey_ps")
-                for half, src, m in ((0, e_bf, n_e), (1, y_bf, n_y)):
-                    if live(m):
-                        words = src[m][:].bitcast(F32)
-                        for u in range(2):
-                            nc.tensor.transpose(ey_ps[:, half, u, :], words[:, u * P : (u + 1) * P], ident[:])
-            if live(n):
-                xt_ps = psum.tile([P, X_PASSES, 2, P], F32, name="xt_ps")
-                words = x_sb[n][:].bitcast(F32)
-                for g in range(X_PASSES):
-                    for u in range(2):
-                        nc.tensor.transpose(
-                            xt_ps[:, g, u, :], words[:, 2 * P * g + u : 2 * P * (g + 1) : 2], ident[:]
-                        )
+        def quantize_x(n):
+            codes = work.tile([P, D // 4], U32, name="x_codes", align_bytes=64)
+            plane = work.tile([P, D // 4], U8, name="x_plane", align_bytes=64)
+            nc.vector.quantize_mx(out=codes[:].bitcast(FP8X4), scales=plane[:], in_=x_grouped[n][:])
+            x_q[n] = (codes, plane)
 
-            m = n - 2
-            if live(m):
-                e_bf[m] = work.tile([P, E], BF16, name="e_bf")
-                nc.scalar.activation(
-                    out=e_bf[m][:].rearrange("p (u m e) -> p u m e", u=2, e=2),
-                    in_=h_ps[m][:].rearrange("p (m u e) -> p u m e", u=2, e=2),
-                    func=ACT.Copy,
-                    scale=row_cols[:, m : m + 1],
-                )
-            y_half_on_vector = live(n_y) and live(n_e) and n % 2 == 0
-            if live(n_e) or live(n_y):
-                turned[n] = work.tile([P, 2, 4 * P], BF16, name="turned", align_bytes=64)
-                lo = 0 if live(n_e) else 1
-                hi = 2 if live(n_y) and not y_half_on_vector else 1
-                nc.scalar.copy(
-                    out=turned[n][:, lo:hi, :].bitcast(F32).rearrange("p h (r u) -> p h r u", u=2),
-                    in_=ey_ps[:, lo:hi].rearrange("p h u r -> p h r u"),
-                )
-            m = n - 6
-            if live(m):
-                y_sb[m] = work.tile([P, C], F32, name="y_sb", bufs=4)
-                nc.scalar.activation(out=y_sb[m][:], in_=z_sb[m][:], func=ACT.Exp)
-                nc.sync.dma_start(out=y_rows[m * P : (m + 1) * P, :], in_=y_sb[m][:])
-            if live(n):
-                x_grouped[n] = work.tile([P, D], BF16, name="x_grouped", align_bytes=64)
-                nc.scalar.copy(
-                    out=x_grouped[n][:].bitcast(F32).rearrange("p (g r u) -> p g r u", g=X_PASSES, u=2),
-                    in_=xt_ps[:].rearrange("p g u r -> p g r u"),
-                )
-
-            m = n - 5
-            if live(m):
-                scaled = work.tile([P, C], F32, name="scaled", bufs=2)
-                nc.vector.tensor_tensor(
-                    out=scaled[:], in0=c_ps[m][:], in1=gain_sb[m // TILES_PER_DOMAIN][:], op=ALU.mult
-                )
-            m = n - 1
-            if live(m):
-                codes = work.tile([P, D // 4], U32, name="x_codes", align_bytes=64)
-                plane = work.tile([P, D // 4], U8, name="x_plane", align_bytes=64)
-                nc.vector.quantize_mx(out=codes[:].bitcast(FP8X4), scales=plane[:], in_=x_grouped[m][:])
-                x_q[m] = (codes, plane)
-            m = n - 5
-            if live(m):
-                z_sb[m] = work.tile([P, C], F32, name="z_sb")
-                nc.vector.scalar_tensor_tensor(
-                    out=z_sb[m][:],
-                    in0=scaled[:],
-                    scalar=row_cols[:, TILES + m : TILES + m + 1],
-                    in1=sine_sb[m // TILES_PER_DOMAIN][:],
-                    op0=ALU.subtract,
-                    op1=ALU.subtract,
-                )
-            m = n - 4
-            if live(m):
-                codes = work.tile([P, P], U32, name="e_codes", align_bytes=64)
-                plane = work.tile([P, P], U8, name="e_plane", align_bytes=64)
-                nc.vector.quantize_mx(out=codes[:].bitcast(FP8X4), scales=plane[:], in_=turned[n - 1][:, 0, :])
-                e_q[m] = (codes, plane)
-            m = n - 8
-            if live(m):
-                group, slot = divmod(m, WORDS_GROUP)
-                if slot == 0:
-                    y_codes[group] = work.tile([P, WORDS_GROUP * P], U32, name="y_codes", align_bytes=64)
-                nc.vector.quantize_mx(
-                    out=y_codes[group][:, slot * P : (slot + 1) * P].bitcast(FP8X4),
-                    scales=y_plane[:, m * P : (m + 1) * P],
-                    in_=turned[n - 1][:, 1, :],
-                )
-                if slot == WORDS_GROUP - 1:
-                    nc.sync.dma_start(
-                        out=y_words32[:, group * WORDS_GROUP * P : (group + 1) * WORDS_GROUP * P],
-                        in_=y_codes[group][:].bitcast(I32),
-                    )
-                if m in SCALE_STORES:
-                    i = SCALE_STORES.index(m)
-                    first = 0 if i == 0 else SCALE_STORES[i - 1] + 1
-                    for q in range(4):
-                        nc.sync.dma_start(
-                            out=y_scales32[4 * q : 4 * q + 4, first * P // 4 : (m + 1) * P // 4],
-                            in_=y_plane[32 * q : 32 * q + 4, first * P : (m + 1) * P].bitcast(I32),
-                        )
-            m = n - 6
-            if live(m):
-                y_bf[m] = work.tile([P, C], BF16, name="y_bf")
-                nc.vector.tensor_copy(
-                    out=y_bf[m][:].rearrange("p (u m e) -> p u m e", u=2, e=2),
-                    in_=y_sb[m][:].rearrange("p (m u e) -> p u m e", u=2, e=2),
-                )
-            if y_half_on_vector:
-                nc.vector.tensor_copy(
-                    out=turned[n][:, 1, :].bitcast(F32).rearrange("p (r u) -> p r u", u=2),
-                    in_=ey_ps[:, 1].rearrange("p u r -> p r u"),
-                )
-
-            m = n - 1
-            if live(m):
-                u = m // TILES_PER_DOMAIN
-                h_ps[m] = psum.tile([P, E], F32, name="h_ps")
-                codes, plane = x_q[m]
-                for g in range(X_PASSES):
-                    nc.tensor.matmul_mx(
-                        out=h_ps[m][:],
-                        lhsT=codes[:, g * P : (g + 1) * P].bitcast(FP8X4),
-                        lhsT_scale=plane[:, g * P : (g + 1) * P],
-                        rhs=w_sb[u][:, g, :].bitcast(FP4X4),
-                        rhs_scale=w_plane[:, X_PASSES * u + g, :],
-                        start=(g == 0),
-                        stop=(g == X_PASSES - 1),
-                    )
-            m = n - 4
-            if live(m):
-                u = m // TILES_PER_DOMAIN
-                c_ps[m] = psum.tile([P, C], F32, name="c_ps")
-                codes, plane = e_q[m]
+        def embed(n):
+            u = n // TILES_PER_DOMAIN
+            h_ps[n] = next_bank([P, E])
+            codes, plane = x_q[n]
+            for g in range(X_PASSES):
                 nc.tensor.matmul_mx(
-                    out=c_ps[m][:],
-                    lhsT=codes[:].bitcast(FP8X4),
-                    lhsT_scale=plane[:],
-                    rhs=v_sb[u][:].bitcast(FP4X4),
-                    rhs_scale=v_plane[:, u, :],
+                    out=h_ps[n][:],
+                    lhsT=codes[:, g * P : (g + 1) * P].bitcast(FP8X4),
+                    lhsT_scale=plane[:, g * P : (g + 1) * P],
+                    rhs=w_sb[u][:, g, :].bitcast(FP4X4),
+                    rhs_scale=w_plane[:, X_PASSES * u + g, :],
+                    start=(g == 0),
+                    stop=(g == X_PASSES - 1),
+                )
+
+        def scale_embedding(n):
+            e_bf[n] = work.tile([P, E], BF16, name="e_bf", bufs=4)
+            nc.scalar.activation(
+                out=e_bf[n][:].rearrange("p (u m e) -> p u m e", u=2, e=2),
+                in_=h_ps[n][:].rearrange("p (m u e) -> p u m e", u=2, e=2),
+                func=ACT.Copy,
+                scale=len_cols[:, n : n + 1],
+            )
+
+        def turn_pair(halves):
+            bank = next_bank([P, 2, 2, P])
+            for i in range(2):
+                words = halves[i].bitcast(F32)
+                for u in range(2):
+                    nc.tensor.transpose(bank[:, i, u, :], words[:, u * P : (u + 1) * P], ident[:])
+            return bank
+
+        def group_pair(copy, bank, name):
+            grouped = work.tile([P, 8 * P], BF16, name=name, bufs=2, align_bytes=64)
+            copy(
+                out=grouped[:].bitcast(F32).rearrange("p (i r u) -> p i r u", i=2, u=2),
+                in_=bank[:].rearrange("p i u r -> p i r u"),
+            )
+            return grouped
+
+        def turn_e(j):
+            e_ps[j] = turn_pair([e_bf[2 * j][:], e_bf[2 * j + 1][:]])
+
+        def group_e(j):
+            e_grouped[j] = group_pair(nc.scalar.copy, e_ps[j], "e_grouped")
+
+        def quantize_e(j):
+            codes = work.tile([P, 2 * P], U32, name="e_codes", align_bytes=64)
+            plane = work.tile([P, 2 * P], U8, name="e_plane", align_bytes=64)
+            nc.vector.quantize_mx(out=codes[:].bitcast(FP8X4), scales=plane[:], in_=e_grouped[j][:])
+            e_q[j] = (codes, plane)
+
+        def similarities(h):
+            j, half = divmod(h, 2)
+            u = 2 * j // TILES_PER_DOMAIN
+            c_ps[h] = next_bank([P, 2, 2 * P])
+            codes, plane = e_q[j]
+            for i in range(2):
+                s = 2 * half + i
+                nc.tensor.matmul_mx(
+                    out=c_ps[h][:, i, :],
+                    lhsT=v_sb[u][:, 2 * P * s : 2 * P * (s + 1)].bitcast(FP4X4),
+                    lhsT_scale=v_plane[:, u, P * s : P * (s + 1)],
+                    rhs=codes[:].bitcast(FP8X4),
+                    rhs_scale=plane[:],
                     start=True,
                     stop=True,
                 )
+
+        def margin_logits(h):
+            j, half = divmod(h, 2)
+            u = 2 * j // TILES_PER_DOMAIN
+            if half == 0:
+                z_sb[j] = work.tile([P, SLICES, 2 * P], F32, name="z_sb")
+            for i in range(2):
+                s = 2 * half + i
+                col = u * SLICES + s
+                gain = gain_cols[:, col : col + 1]
+                neg_sine = neg_cols[:, TILES + col : TILES + col + 1]
+                if h >= SCALAR_LOGITS_FROM and half == 1:
+                    nc.scalar.activation(
+                        out=z_sb[j][:, s, :], in_=c_ps[h][:, i, :], func=ACT.Identity, scale=gain, bias=neg_sine
+                    )
+                else:
+                    nc.vector.tensor_scalar(
+                        out=z_sb[j][:, s, :],
+                        in0=c_ps[h][:, i, :],
+                        scalar1=gain,
+                        scalar2=neg_sine,
+                        op0=ALU.mult,
+                        op1=ALU.add,
+                    )
+
+        def turn_z(n):
+            j, i = divmod(n, 2)
+            z_ps[n] = next_bank([P, SLICES, P])
+            for s in range(SLICES):
+                nc.tensor.transpose(z_ps[n][:, s, :], z_sb[j][:, s, i * P : (i + 1) * P], ident[:])
+
+        def exponentiate(n):
+            j, i = divmod(n, 2)
+            if i == 0:
+                y_sb[j] = work.tile([P, 2, C], F32, name="y_sb")
+            nc.scalar.activation(
+                out=y_sb[j][:, i, :],
+                in_=z_ps[n][:].rearrange("p s m -> p (s m)"),
+                func=ACT.Exp,
+                bias=neg_cols[:, n : n + 1],
+            )
+            nc.sync.dma_start(out=y_rows[n * P : (n + 1) * P, :], in_=y_sb[j][:, i, :])
+
+        def round_y(j):
+            y_bf[j] = work.tile([P, 2, C], BF16, name="y_bf", bufs=2)
+            nc.vector.tensor_copy(
+                out=y_bf[j][:].rearrange("p i (u m e) -> p i u m e", u=2, e=2),
+                in_=y_sb[j][:].rearrange("p i (m u e) -> p i u m e", u=2, e=2),
+            )
+
+        def turn_y(j):
+            y_ps[j] = turn_pair([y_bf[j][:, 0, :], y_bf[j][:, 1, :]])
+
+        def group_y(j):
+            copy = nc.scalar.copy if j >= SCALAR_GROUPS_FROM else nc.vector.tensor_copy
+            y_grouped[j] = group_pair(copy, y_ps[j], "y_grouped")
+
+        def quantize_y(j):
+            cols = slice(2 * P * j, 2 * P * (j + 1))
+            codes = work.tile([P, 2 * P], U32, name="y_codes", align_bytes=64)
+            nc.vector.quantize_mx(out=codes[:].bitcast(FP8X4), scales=y_plane[:, cols], in_=y_grouped[j][:])
+            nc.sync.dma_start(out=y_words32[:, cols], in_=codes[:].bitcast(I32))
+            if j in SCALE_STORES:
+                i = SCALE_STORES.index(j)
+                first = 0 if i == 0 else 2 * P * (SCALE_STORES[i - 1] + 1)
+                for q in range(4):
+                    nc.sync.dma_start(
+                        out=y_scales32[4 * q : 4 * q + 4, first // 4 : cols.stop // 4],
+                        in_=y_plane[32 * q : 32 * q + 4, first : cols.stop].bitcast(I32),
+                    )
+
+        nc.vector.memset(w_plane[:].bitcast(I32), 0)
+        nc.vector.memset(warm[:], 0.0)
+        nc.vector.memset(len_rows32[:], 0.0)
+        nc.vector.memset(late_rows32[:], 0.0)
+        nc.vector.memset(v_plane[:].bitcast(I32), 0)
+        nc.scalar.activation(out=warm_out[:], in_=warm[:], func=ACT.Exp)
+        make_identity(nc, ident[:])
+        load_x_tile(0)
+        load_w(0)
+        load_plane(w_plane, w_scales32)
+        load_x_tile(1)
+        nc.sync.dma_start(out=len_rows[:TILES, :], in_=len_scale.rearrange("g (n p) -> (g n) p", p=P))
+        load_x_pair(1)
+        load_x_pair(2)
+        nc.sync.dma_start(out=late_rows[:TILES, :], in_=shift.rearrange("g (n p) -> (g n) p", p=P))
+        nc.sync.dma_start(out=late_rows[48:64, :], in_=cos_gain.rearrange("g (s p) -> (g s) p", p=P))
+        nc.sync.dma_start(out=late_rows[32:48, :], in_=sine_term.rearrange("g (s p) -> (g s) p", p=P))
+        load_v(0)
+        load_plane(v_plane, v_scales32)
+
+        def per_tile(stage, n, lag):
+            if 0 <= n - lag < TILES:
+                stage(n - lag)
+
+        def per_pair(stage, n, lag):
+            if (n - lag) % 2 == 0 and 0 <= n - lag < TILES:
+                stage((n - lag) // 2)
+
+        for n in range(TILES + 12):
+            per_pair(load_x_pair, n, -X_LEAD)
+            u_next, phase = divmod(n + TILES_PER_DOMAIN, TILES_PER_DOMAIN)
+            if u_next < G and phase == 4:
+                load_w(u_next)
+            if u_next < G and phase == 7:
+                load_v(u_next)
+
+            per_tile(turn_z, n, 8)
+            per_tile(turn_x, n, 0)
+            per_pair(turn_e, n, 4)
+            per_pair(turn_y, n, 11)
+
+            per_tile(scale_embedding, n, 2)
+            per_tile(exponentiate, n, 8)
+            per_tile(group_x, n, 0)
+            per_pair(group_e, n, 4)
+
+            per_tile(quantize_x, n, 1)
+            per_pair(quantize_e, n, 5)
+            per_tile(margin_logits, n, 6)
+            per_pair(round_y, n, 10)
+            per_pair(quantize_y, n, 12)
+            per_pair(group_y, n, 11)
+            if n == 1:
+                turn_len_scale()
+            if n == 3:
+                turn_late_vectors()
+
+            per_tile(embed, n, 1)
+            per_tile(similarities, n, 5)

@@ -21,12 +21,17 @@ K_PASS = 512
 TILES = G * R // P
 TILES_PER_DOMAIN = R // P
 X_PASSES = D // K_PASS
-X_LEAD = 6
+X_LEAD = 4
 PAIRS = TILES // 2
 SLICES = C // P
-SCALE_STORES = (7, 13, 15)
+PAIRS_PER_DOMAIN = TILES_PER_DOMAIN // 2
+SCALE_STORES = (7, 11, 15)
 PSUM_BANKS = 8
-SCALAR_LOGITS_FROM = 99
+SORT_X_FROM = 2
+SORT_X_UNTIL = 0
+VECTOR_GROUPS_X_UNTIL = 4
+E_ON_VECTOR_EVERY = 4
+SCALAR_LOGITS_FROM = 26
 SCALAR_GROUPS_FROM = 11
 
 
@@ -54,10 +59,9 @@ def tile_domain_margin_softmax_weights_k7_kernel(
         v_plane = keep.tile([P, G, C], U8, name="v_plane", align_bytes=64)
         y_plane = keep.tile([P, G * R], U8, name="y_plane", align_bytes=64)
         len_rows = keep.tile([P, P], BF16, name="len_rows")
-        len_rows32 = keep.tile([P, P], F32, name="len_rows32")
         len_cols = keep.tile([P, TILES], F32, name="len_cols")
         late_rows = keep.tile([P, P], BF16, name="late_rows")
-        late_rows32 = keep.tile([P, P], F32, name="late_rows32")
+        ident_bf = keep.tile([P, P], BF16, name="ident_bf")
         neg_cols = keep.tile([P, TILES + G * SLICES], F32, name="neg_cols")
         gain_cols = keep.tile([P, G * SLICES], F32, name="gain_cols")
         warm = keep.tile([P, 1], F32, name="warm")
@@ -65,10 +69,11 @@ def tile_domain_margin_softmax_weights_k7_kernel(
 
         x_sb, x_ps, x_grouped, x_q, h_ps, e_bf, e_ps, e_grouped, e_q = ({} for i in range(9))
         c_ps, z_sb, z_ps, y_sb, y_bf, y_ps, y_grouped, w_sb, v_sb = ({} for i in range(9))
+        x_sorted = {}
         banks_used = []
 
-        def next_bank(shape):
-            bank = psum.tile(shape, F32, name="bank%d" % (len(banks_used) % PSUM_BANKS))
+        def next_bank(shape, dtype=F32):
+            bank = psum.tile(shape, dtype, name="bank%d" % (len(banks_used) % PSUM_BANKS))
             banks_used.append(bank)
             return bank
 
@@ -78,7 +83,7 @@ def tile_domain_margin_softmax_weights_k7_kernel(
             x_sb[n] = first[:]
 
         def load_x_pair(j):
-            pair = work.tile([P, 2, D], BF16, name="x_pair", bufs=4)
+            pair = work.tile([P, 2, D], BF16, name="x_pair", bufs=5)
             nc.sync.dma_start(out=pair[:], in_=x_rows[2 * P * j : 2 * P * (j + 1), :].rearrange("(i p) d -> p i d", p=P))
             x_sb[2 * j] = pair[:, 0, :]
             x_sb[2 * j + 1] = pair[:, 1, :]
@@ -101,16 +106,17 @@ def tile_domain_margin_softmax_weights_k7_kernel(
                     in_=scales32[:, 4 * q : 4 * q + 4, :].rearrange("g r n -> r g n"),
                 )
 
+        def turn_rows(rows):
+            bank = next_bank([P, P], BF16)
+            nc.tensor.transpose(bank[:], rows[:], ident_bf[:])
+            return bank
+
         def turn_len_scale():
-            nc.vector.tensor_copy(out=len_rows32[:TILES, :], in_=len_rows[:TILES, :])
-            bank = next_bank([P, P])
-            nc.tensor.transpose(bank[:], len_rows32[:], ident[:])
-            nc.vector.tensor_copy(out=len_cols[:], in_=bank[:, :TILES])
+            bank = turn_rows(len_rows)
+            nc.scalar.copy(out=len_cols[:], in_=bank[:, :TILES])
 
         def turn_late_vectors():
-            nc.vector.tensor_copy(out=late_rows32[: 2 * TILES, :], in_=late_rows[: 2 * TILES, :])
-            bank = next_bank([P, P])
-            nc.tensor.transpose(bank[:], late_rows32[:], ident[:])
+            bank = turn_rows(late_rows)
             nc.vector.tensor_scalar(
                 out=neg_cols[:], in0=bank[:, : TILES + G * SLICES], scalar1=-1.0, scalar2=None, op0=ALU.mult
             )
@@ -121,30 +127,45 @@ def tile_domain_margin_softmax_weights_k7_kernel(
             words = x_sb[n].bitcast(F32)
             for g in range(X_PASSES):
                 for u in range(2):
-                    nc.tensor.transpose(x_ps[n][:, g, u, :], words[:, 2 * P * g + u : 2 * P * (g + 1) : 2], ident[:])
+                    if n in x_sorted:
+                        src = x_sorted[n][:, g, u, :]
+                    else:
+                        src = words[:, 2 * P * g + u : 2 * P * (g + 1) : 2]
+                    nc.tensor.transpose(x_ps[n][:, g, u, :], src, ident[:])
+
+        def sort_x(n):
+            words = work.tile([P, X_PASSES, 2, P], F32, name="x_sorted", bufs=4)
+            nc.vector.tensor_copy(
+                out=words[:], in_=x_sb[n].bitcast(F32).rearrange("p (g m u) -> p g u m", g=X_PASSES, u=2)
+            )
+            x_sorted[n] = words
 
         def group_x(n):
-            x_grouped[n] = work.tile([P, D], BF16, name="x_grouped", align_bytes=64)
-            nc.scalar.copy(
-                out=x_grouped[n][:].bitcast(F32).rearrange("p (g r u) -> p g r u", g=X_PASSES, u=2),
+            j, i = divmod(n, 2)
+            if i == 0:
+                x_grouped[j] = work.tile([P, 2 * D], BF16, name="x_grouped", bufs=2, align_bytes=64)
+            copy = nc.vector.tensor_copy if i == 1 and j < VECTOR_GROUPS_X_UNTIL else nc.scalar.copy
+            copy(
+                out=x_grouped[j][:, i * D : (i + 1) * D].bitcast(F32).rearrange("p (g r u) -> p g r u", g=X_PASSES, u=2),
                 in_=x_ps[n][:].rearrange("p g u r -> p g r u"),
             )
 
-        def quantize_x(n):
-            codes = work.tile([P, D // 4], U32, name="x_codes", align_bytes=64)
-            plane = work.tile([P, D // 4], U8, name="x_plane", align_bytes=64)
-            nc.vector.quantize_mx(out=codes[:].bitcast(FP8X4), scales=plane[:], in_=x_grouped[n][:])
-            x_q[n] = (codes, plane)
+        def quantize_x(j):
+            codes = work.tile([P, 2 * D // 4], U32, name="x_codes", bufs=2, align_bytes=64)
+            plane = work.tile([P, 2 * D // 4], U8, name="x_plane", bufs=2, align_bytes=64)
+            nc.vector.quantize_mx(out=codes[:].bitcast(FP8X4), scales=plane[:], in_=x_grouped[j][:])
+            x_q[j] = (codes, plane)
 
         def embed(n):
             u = n // TILES_PER_DOMAIN
             h_ps[n] = next_bank([P, E])
-            codes, plane = x_q[n]
+            codes, plane = x_q[n // 2]
             for g in range(X_PASSES):
+                first = (n % 2 * X_PASSES + g) * P
                 nc.tensor.matmul_mx(
                     out=h_ps[n][:],
-                    lhsT=codes[:, g * P : (g + 1) * P].bitcast(FP8X4),
-                    lhsT_scale=plane[:, g * P : (g + 1) * P],
+                    lhsT=codes[:, first : first + P].bitcast(FP8X4),
+                    lhsT_scale=plane[:, first : first + P],
                     rhs=w_sb[u][:, g, :].bitcast(FP4X4),
                     rhs_scale=w_plane[:, X_PASSES * u + g, :],
                     start=(g == 0),
@@ -180,7 +201,8 @@ def tile_domain_margin_softmax_weights_k7_kernel(
             e_ps[j] = turn_pair([e_bf[2 * j][:], e_bf[2 * j + 1][:]])
 
         def group_e(j):
-            e_grouped[j] = group_pair(nc.scalar.copy, e_ps[j], "e_grouped")
+            copy = nc.vector.tensor_copy if j % E_ON_VECTOR_EVERY == E_ON_VECTOR_EVERY - 1 else nc.scalar.copy
+            e_grouped[j] = group_pair(copy, e_ps[j], "e_grouped")
 
         def quantize_e(j):
             codes = work.tile([P, 2 * P], U32, name="e_codes", align_bytes=64)
@@ -277,60 +299,66 @@ def tile_domain_margin_softmax_weights_k7_kernel(
 
         nc.vector.memset(w_plane[:].bitcast(I32), 0)
         nc.vector.memset(warm[:], 0.0)
-        nc.vector.memset(len_rows32[:], 0.0)
-        nc.vector.memset(late_rows32[:], 0.0)
+        nc.vector.memset(len_rows[TILES : 2 * TILES, :], 0.0)
+        nc.vector.memset(len_rows[2 * TILES :, :], 0.0)
+        nc.vector.memset(late_rows[2 * TILES :, :], 0.0)
         nc.vector.memset(v_plane[:].bitcast(I32), 0)
         nc.scalar.activation(out=warm_out[:], in_=warm[:], func=ACT.Exp)
         make_identity(nc, ident[:])
+        make_identity(nc, ident_bf[:])
         load_x_tile(0)
+        load_x_tile(1)
+        load_x_pair(1)
         load_w(0)
         load_plane(w_plane, w_scales32)
-        load_x_tile(1)
         nc.sync.dma_start(out=len_rows[:TILES, :], in_=len_scale.rearrange("g (n p) -> (g n) p", p=P))
-        load_x_pair(1)
         load_x_pair(2)
+        load_x_pair(3)
         nc.sync.dma_start(out=late_rows[:TILES, :], in_=shift.rearrange("g (n p) -> (g n) p", p=P))
         nc.sync.dma_start(out=late_rows[48:64, :], in_=cos_gain.rearrange("g (s p) -> (g s) p", p=P))
         nc.sync.dma_start(out=late_rows[32:48, :], in_=sine_term.rearrange("g (s p) -> (g s) p", p=P))
         load_v(0)
         load_plane(v_plane, v_scales32)
 
-        def per_tile(stage, n, lag):
-            if 0 <= n - lag < TILES:
-                stage(n - lag)
+        def per_pair(stage, j):
+            if 0 <= j < PAIRS:
+                stage(j)
 
-        def per_pair(stage, n, lag):
-            if (n - lag) % 2 == 0 and 0 <= n - lag < TILES:
-                stage((n - lag) // 2)
+        def both_tiles(stage, j):
+            if 0 <= j < PAIRS:
+                stage(2 * j)
+                stage(2 * j + 1)
 
-        for n in range(TILES + 12):
-            per_pair(load_x_pair, n, -X_LEAD)
-            u_next, phase = divmod(n + TILES_PER_DOMAIN, TILES_PER_DOMAIN)
-            if u_next < G and phase == 4:
+        for k in range(PAIRS + 7):
+            per_pair(load_x_pair, k + X_LEAD)
+            u_next, phase = divmod(k + PAIRS_PER_DOMAIN, PAIRS_PER_DOMAIN)
+            if u_next < G and phase == 2:
                 load_w(u_next)
-            if u_next < G and phase == 7:
+            if u_next < G and phase == 3:
                 load_v(u_next)
 
-            per_tile(turn_z, n, 8)
-            per_tile(turn_x, n, 0)
-            per_pair(turn_e, n, 4)
-            per_pair(turn_y, n, 11)
+            both_tiles(scale_embedding, k - 2)
 
-            per_tile(scale_embedding, n, 2)
-            per_tile(exponentiate, n, 8)
-            per_tile(group_x, n, 0)
-            per_pair(group_e, n, 4)
+            both_tiles(turn_z, k - 5)
+            both_tiles(turn_x, k)
+            per_pair(turn_e, k - 2)
+            per_pair(turn_y, k - 6)
 
-            per_tile(quantize_x, n, 1)
-            per_pair(quantize_e, n, 5)
-            per_tile(margin_logits, n, 6)
-            per_pair(round_y, n, 10)
-            per_pair(quantize_y, n, 12)
-            per_pair(group_y, n, 11)
-            if n == 1:
+            per_pair(quantize_x, k - 1)
+            both_tiles(exponentiate, k - 5)
+            both_tiles(margin_logits, k - 4)
+            per_pair(quantize_e, k - 3)
+            per_pair(round_y, k - 5)
+            per_pair(quantize_y, k - 7)
+            both_tiles(group_x, k)
+            if k == 1:
                 turn_len_scale()
-            if n == 3:
+            if k == 2:
                 turn_late_vectors()
+            per_pair(group_y, k - 6)
+            per_pair(group_e, k - 2)
+            if SORT_X_FROM <= k + 1 < SORT_X_UNTIL:
+                both_tiles(sort_x, k + 1)
 
-            per_tile(embed, n, 1)
-            per_tile(similarities, n, 5)
+            both_tiles(embed, k - 1)
+            both_tiles(similarities, k - 3)

@@ -27,11 +27,13 @@ SLICES = C // P
 PAIRS_PER_DOMAIN = TILES_PER_DOMAIN // 2
 SCALE_STORES = (7, 11, 15)
 PSUM_BANKS = 8
+GPSIMD_ROUNDS_UNTIL = 14
+SORT_EVERY = 1
 SORT_X_FROM = 2
 SORT_X_UNTIL = 0
-VECTOR_GROUPS_X_UNTIL = 4
-E_ON_VECTOR_EVERY = 4
-SCALAR_LOGITS_FROM = 26
+VECTOR_GROUPS_X_UNTIL = 0
+E_ON_VECTOR_EVERY = 2
+SCALAR_LOGITS_FROM = 99
 SCALAR_GROUPS_FROM = 11
 
 
@@ -64,8 +66,6 @@ def tile_domain_margin_softmax_weights_k7_kernel(
         ident_bf = keep.tile([P, P], BF16, name="ident_bf")
         neg_cols = keep.tile([P, TILES + G * SLICES], F32, name="neg_cols")
         gain_cols = keep.tile([P, G * SLICES], F32, name="gain_cols")
-        warm = keep.tile([P, 1], F32, name="warm")
-        warm_out = keep.tile([P, 1], F32, name="warm_out")
 
         x_sb, x_ps, x_grouped, x_q, h_ps, e_bf, e_ps, e_grouped, e_q = ({} for i in range(9))
         c_ps, z_sb, z_ps, y_sb, y_bf, y_ps, y_grouped, w_sb, v_sb = ({} for i in range(9))
@@ -271,10 +271,22 @@ def tile_domain_margin_softmax_weights_k7_kernel(
 
         def round_y(j):
             y_bf[j] = work.tile([P, 2, C], BF16, name="y_bf", bufs=2)
-            nc.vector.tensor_copy(
-                out=y_bf[j][:].rearrange("p i (u m e) -> p i u m e", u=2, e=2),
-                in_=y_sb[j][:].rearrange("p i (m u e) -> p i u m e", u=2, e=2),
-            )
+            if j < GPSIMD_ROUNDS_UNTIL:
+                for i in range(2):
+                    nc.gpsimd.tensor_scalar(
+                        out=y_bf[j][:, i, :].rearrange("p (u m e) -> p u m e", u=2, e=2),
+                        in0=y_sb[j][:, i, :].rearrange("p (m u e) -> p u m e", u=2, e=2),
+                        scalar1=1.0,
+                        scalar2=0.0,
+                        op0=ALU.mult,
+                        op1=ALU.add,
+                    )
+            else:
+                for i in range(2):
+                    nc.vector.tensor_copy(
+                        out=y_bf[j][:, i, :].rearrange("p (u m e) -> p u m e", u=2, e=2),
+                        in_=y_sb[j][:, i, :].rearrange("p (m u e) -> p u m e", u=2, e=2),
+                    )
 
         def turn_y(j):
             y_ps[j] = turn_pair([y_bf[j][:, 0, :], y_bf[j][:, 1, :]])
@@ -298,14 +310,12 @@ def tile_domain_margin_softmax_weights_k7_kernel(
                     )
 
         nc.vector.memset(w_plane[:].bitcast(I32), 0)
-        nc.vector.memset(warm[:], 0.0)
         nc.vector.memset(len_rows[TILES : 2 * TILES, :], 0.0)
         nc.vector.memset(len_rows[2 * TILES :, :], 0.0)
         nc.vector.memset(late_rows[2 * TILES :, :], 0.0)
         nc.vector.memset(v_plane[:].bitcast(I32), 0)
-        nc.scalar.activation(out=warm_out[:], in_=warm[:], func=ACT.Exp)
         make_identity(nc, ident[:])
-        make_identity(nc, ident_bf[:])
+        nc.scalar.activation(out=ident_bf[:], in_=ident[:], func=ACT.Copy)
         load_x_tile(0)
         load_x_tile(1)
         load_x_pair(1)
@@ -346,10 +356,12 @@ def tile_domain_margin_softmax_weights_k7_kernel(
 
             per_pair(quantize_x, k - 1)
             both_tiles(exponentiate, k - 5)
-            both_tiles(margin_logits, k - 4)
             per_pair(quantize_e, k - 3)
-            per_pair(round_y, k - 5)
             per_pair(quantize_y, k - 7)
+            if 1 <= k < PAIRS - 1 and k % SORT_EVERY == 0:
+                sort_x(2 * k + 3)
+            both_tiles(margin_logits, k - 4)
+            per_pair(round_y, k - 5)
             both_tiles(group_x, k)
             if k == 1:
                 turn_len_scale()
@@ -358,7 +370,7 @@ def tile_domain_margin_softmax_weights_k7_kernel(
             per_pair(group_y, k - 6)
             per_pair(group_e, k - 2)
             if SORT_X_FROM <= k + 1 < SORT_X_UNTIL:
-                both_tiles(sort_x, k + 1)
+                sort_x(2 * k + 2)
 
             both_tiles(embed, k - 1)
             both_tiles(similarities, k - 3)

from contextlib import ExitStack

import concourse.mybir as mybir
from concourse.masks import make_identity

G, R, D, E, C = 4, 1024, 1024, 512, 512
FLOPS = 2 * G * R * (D * E + E * C)

F32 = mybir.dt.float32
BF16 = mybir.dt.bfloat16
I32 = mybir.dt.int32
U32 = mybir.dt.uint32
U8 = mybir.dt.uint8
FP8X4 = mybir.dt.float8_e4m3fn_x4
FP4X4 = mybir.dt.float4_e2m1fn_x4
ACT = mybir.ActivationFunctionType
ALU = mybir.AluOpType

P = 128
K_PASS = 512
TILES = G * R // P
TILES_PER_DOMAIN = R // P
X_PASSES = D // K_PASS
X_LEAD = 4
PAIRS = TILES // 2
SLICES = C // P
PAIRS_PER_DOMAIN = TILES_PER_DOMAIN // 2
SCALE_STORES = (7, 11, 15)
PSUM_BANKS = 8
GPSIMD_ROUNDS_UNTIL = 14
SORT_EVERY = 1
SORT_X_FROM = 2
SORT_X_UNTIL = 0
VECTOR_GROUPS_X_UNTIL = 0
E_ON_VECTOR_EVERY = 2
SCALAR_LOGITS_FROM = 99
SCALAR_GROUPS_FROM = 11


def tile_domain_margin_softmax_weights_k7_kernel(
    tc, x, w_words, w_scales, v_words, v_scales, len_scale, cos_gain, sine_term, shift, out_0, out_1, out_2
):
    nc = tc.nc
    x_rows = x.rearrange("g r d -> (g r) d")
    y_rows = out_0.rearrange("g r c -> (g r) c")
    w_words32 = w_words.bitcast(I32)
    v_words32 = v_words.bitcast(I32)
    w_scales32 = w_scales.bitcast(I32)
    v_scales32 = v_scales.bitcast(I32)
    y_words32 = out_1[0].rearrange("p m t -> p (m t)").bitcast(I32)
    y_scales32 = out_2[0].bitcast(I32)

    with ExitStack() as ctx:
        keep = ctx.enter_context(tc.tile_pool(name="keep", bufs=1))
        work = ctx.enter_context(tc.tile_pool(name="work", bufs=3))
        psum = ctx.enter_context(tc.psum_pool(name="psum", bufs=1))
        ctx.enter_context(tc.manual_schedule())

        ident = keep.tile([P, P], F32, name="ident")
        w_plane = keep.tile([P, G * X_PASSES, E], U8, name="w_plane", align_bytes=64)
        v_plane = keep.tile([P, G, C], U8, name="v_plane", align_bytes=64)
        y_plane = keep.tile([P, G * R], U8, name="y_plane", align_bytes=64)
        len_rows = keep.tile([P, P], BF16, name="len_rows")
        len_cols = keep.tile([P, TILES], F32, name="len_cols")
        late_rows = keep.tile([P, P], BF16, name="late_rows")
        ident_bf = keep.tile([P, P], BF16, name="ident_bf")
        neg_cols = keep.tile([P, TILES + G * SLICES], F32, name="neg_cols")
        gain_cols = keep.tile([P, G * SLICES], F32, name="gain_cols")

        x_sb, x_ps, x_grouped, x_q, h_ps, e_bf, e_ps, e_grouped, e_q = ({} for i in range(9))
        c_ps, z_sb, z_ps, y_sb, y_bf, y_ps, y_grouped, w_sb, v_sb = ({} for i in range(9))
        x_sorted = {}
        banks_used = []

        def next_bank(shape, dtype=F32):
            bank = psum.tile(shape, dtype, name="bank%d" % (len(banks_used) % PSUM_BANKS))
            banks_used.append(bank)
            return bank

        def load_x_tile(n):
            first = keep.tile([P, D], BF16, name="x_first%d" % n)
            nc.sync.dma_start(out=first[:], in_=x_rows[n * P : (n + 1) * P, :])
            x_sb[n] = first[:]

        def load_x_pair(j):
            pair = work.tile([P, 2, D], BF16, name="x_pair", bufs=5)
            nc.sync.dma_start(out=pair[:], in_=x_rows[2 * P * j : 2 * P * (j + 1), :].rearrange("(i p) d -> p i d", p=P))
            x_sb[2 * j] = pair[:, 0, :]
            x_sb[2 * j + 1] = pair[:, 1, :]

        def load_w(u):
            w_sb[u] = work.tile([P, X_PASSES, 2 * E], U8, name="w_sb", bufs=2, align_bytes=64)
            nc.sync.dma_start(
                out=w_sb[u][:].bitcast(I32),
                in_=w_words32[X_PASSES * u : X_PASSES * (u + 1)].rearrange("g p n -> p g n"),
            )

        def load_v(u):
            v_sb[u] = work.tile([P, 2 * C], U8, name="v_sb", bufs=2, align_bytes=64)
            nc.sync.dma_start(out=v_sb[u][:].bitcast(I32), in_=v_words32[u])

        def load_plane(plane, scales32):
            for q in range(4):
                nc.sync.dma_start(
                    out=plane[32 * q : 32 * q + 4].bitcast(I32),
                    in_=scales32[:, 4 * q : 4 * q + 4, :].rearrange("g r n -> r g n"),
                )

        def turn_rows(rows):
            bank = next_bank([P, P], BF16)
            nc.tensor.transpose(bank[:], rows[:], ident_bf[:])
            return bank

        def turn_len_scale():
            bank = turn_rows(len_rows)
            nc.scalar.copy(out=len_cols[:], in_=bank[:, :TILES])

        def turn_late_vectors():
            bank = turn_rows(late_rows)
            nc.vector.tensor_scalar(
                out=neg_cols[:], in0=bank[:, : TILES + G * SLICES], scalar1=-1.0, scalar2=None, op0=ALU.mult
            )
            nc.vector.tensor_copy(out=gain_cols[:], in_=bank[:, TILES + G * SLICES : 2 * TILES])

        def turn_x(n):
            x_ps[n] = next_bank([P, X_PASSES, 2, P])
            words = x_sb[n].bitcast(F32)
            for g in range(X_PASSES):
                for u in range(2):
                    if n in x_sorted:
                        src = x_sorted[n][:, g, u, :]
                    else:
                        src = words[:, 2 * P * g + u : 2 * P * (g + 1) : 2]
                    nc.tensor.transpose(x_ps[n][:, g, u, :], src, ident[:])

        def sort_x(n):
            words = work.tile([P, X_PASSES, 2, P], F32, name="x_sorted", bufs=4)
            nc.vector.tensor_copy(
                out=words[:], in_=x_sb[n].bitcast(F32).rearrange("p (g m u) -> p g u m", g=X_PASSES, u=2)
            )
            x_sorted[n] = words

        def group_x(n):
            j, i = divmod(n, 2)
            if i == 0:
                x_grouped[j] = work.tile([P, 2 * D], BF16, name="x_grouped", bufs=2, align_bytes=64)
            copy = nc.vector.tensor_copy if i == 1 and j < VECTOR_GROUPS_X_UNTIL else nc.scalar.copy
            copy(
                out=x_grouped[j][:, i * D : (i + 1) * D].bitcast(F32).rearrange("p (g r u) -> p g r u", g=X_PASSES, u=2),
                in_=x_ps[n][:].rearrange("p g u r -> p g r u"),
            )

        def quantize_x(j):
            codes = work.tile([P, 2 * D // 4], U32, name="x_codes", bufs=2, align_bytes=64)
            plane = work.tile([P, 2 * D // 4], U8, name="x_plane", bufs=2, align_bytes=64)
            nc.vector.quantize_mx(out=codes[:].bitcast(FP8X4), scales=plane[:], in_=x_grouped[j][:])
            x_q[j] = (codes, plane)

        def embed(n):
            u = n // TILES_PER_DOMAIN
            h_ps[n] = next_bank([P, E])
            codes, plane = x_q[n // 2]
            for g in range(X_PASSES):
                first = (n % 2 * X_PASSES + g) * P
                nc.tensor.matmul_mx(
                    out=h_ps[n][:],
                    lhsT=codes[:, first : first + P].bitcast(FP8X4),
                    lhsT_scale=plane[:, first : first + P],
                    rhs=w_sb[u][:, g, :].bitcast(FP4X4),
                    rhs_scale=w_plane[:, X_PASSES * u + g, :],
                    start=(g == 0),
                    stop=(g == X_PASSES - 1),
                )

        def scale_embedding(n):
            e_bf[n] = work.tile([P, E], BF16, name="e_bf", bufs=4)
            nc.scalar.activation(
                out=e_bf[n][:].rearrange("p (u m e) -> p u m e", u=2, e=2),
                in_=h_ps[n][:].rearrange("p (m u e) -> p u m e", u=2, e=2),
                func=ACT.Copy,
                scale=len_cols[:, n : n + 1],
            )

        def turn_pair(halves):
            bank = next_bank([P, 2, 2, P])
            for i in range(2):
                words = halves[i].bitcast(F32)
                for u in range(2):
                    nc.tensor.transpose(bank[:, i, u, :], words[:, u * P : (u + 1) * P], ident[:])
            return bank

        def group_pair(copy, bank, name):
            grouped = work.tile([P, 8 * P], BF16, name=name, bufs=2, align_bytes=64)
            copy(
                out=grouped[:].bitcast(F32).rearrange("p (i r u) -> p i r u", i=2, u=2),
                in_=bank[:].rearrange("p i u r -> p i r u"),
            )
            return grouped

        def turn_e(j):
            e_ps[j] = turn_pair([e_bf[2 * j][:], e_bf[2 * j + 1][:]])

        def group_e(j):
            copy = nc.vector.tensor_copy if j % E_ON_VECTOR_EVERY == E_ON_VECTOR_EVERY - 1 else nc.scalar.copy
            e_grouped[j] = group_pair(copy, e_ps[j], "e_grouped")

        def quantize_e(j):
            codes = work.tile([P, 2 * P], U32, name="e_codes", align_bytes=64)
            plane = work.tile([P, 2 * P], U8, name="e_plane", align_bytes=64)
            nc.vector.quantize_mx(out=codes[:].bitcast(FP8X4), scales=plane[:], in_=e_grouped[j][:])
            e_q[j] = (codes, plane)

        def similarities(h):
            j, half = divmod(h, 2)
            u = 2 * j // TILES_PER_DOMAIN
            c_ps[h] = next_bank([P, 2, 2 * P])
            codes, plane = e_q[j]
            for i in range(2):
                s = 2 * half + i
                nc.tensor.matmul_mx(
                    out=c_ps[h][:, i, :],
                    lhsT=v_sb[u][:, 2 * P * s : 2 * P * (s + 1)].bitcast(FP4X4),
                    lhsT_scale=v_plane[:, u, P * s : P * (s + 1)],
                    rhs=codes[:].bitcast(FP8X4),
                    rhs_scale=plane[:],
                    start=True,
                    stop=True,
                )

        def margin_logits(h):
            j, half = divmod(h, 2)
            u = 2 * j // TILES_PER_DOMAIN
            if half == 0:
                z_sb[j] = work.tile([P, SLICES, 2 * P], F32, name="z_sb")
            for i in range(2):
                s = 2 * half + i
                col = u * SLICES + s
                gain = gain_cols[:, col : col + 1]
                neg_sine = neg_cols[:, TILES + col : TILES + col + 1]
                if h >= SCALAR_LOGITS_FROM and half == 1:
                    nc.scalar.activation(
                        out=z_sb[j][:, s, :], in_=c_ps[h][:, i, :], func=ACT.Identity, scale=gain, bias=neg_sine
                    )
                else:
                    nc.vector.tensor_scalar(
                        out=z_sb[j][:, s, :],
                        in0=c_ps[h][:, i, :],
                        scalar1=gain,
                        scalar2=neg_sine,
                        op0=ALU.mult,
                        op1=ALU.add,
                    )

        def turn_z(n):
            j, i = divmod(n, 2)
            z_ps[n] = next_bank([P, SLICES, P])
            for s in range(SLICES):
                nc.tensor.transpose(z_ps[n][:, s, :], z_sb[j][:, s, i * P : (i + 1) * P], ident[:])

        def exponentiate(n):
            j, i = divmod(n, 2)
            if i == 0:
                y_sb[j] = work.tile([P, 2, C], F32, name="y_sb")
            nc.scalar.activation(
                out=y_sb[j][:, i, :],
                in_=z_ps[n][:].rearrange("p s m -> p (s m)"),
                func=ACT.Exp,
                bias=neg_cols[:, n : n + 1],
            )
            nc.sync.dma_start(out=y_rows[n * P : (n + 1) * P, :], in_=y_sb[j][:, i, :])

        def round_y(j):
            y_bf[j] = work.tile([P, 2, C], BF16, name="y_bf", bufs=2)
            if j < GPSIMD_ROUNDS_UNTIL:
                for i in range(2):
                    nc.gpsimd.tensor_scalar(
                        out=y_bf[j][:, i, :].rearrange("p (u m e) -> p u m e", u=2, e=2),
                        in0=y_sb[j][:, i, :].rearrange("p (m u e) -> p u m e", u=2, e=2),
                        scalar1=1.0,
                        scalar2=0.0,
                        op0=ALU.mult,
                        op1=ALU.add,
                    )
            else:
                for i in range(2):
                    nc.vector.tensor_copy(
                        out=y_bf[j][:, i, :].rearrange("p (u m e) -> p u m e", u=2, e=2),
                        in_=y_sb[j][:, i, :].rearrange("p (m u e) -> p u m e", u=2, e=2),
                    )

        def turn_y(j):
            y_ps[j] = turn_pair([y_bf[j][:, 0, :], y_bf[j][:, 1, :]])

        def group_y(j):
            copy = nc.scalar.copy if j >= SCALAR_GROUPS_FROM else nc.vector.tensor_copy
            y_grouped[j] = group_pair(copy, y_ps[j], "y_grouped")

        def quantize_y(j):
            cols = slice(2 * P * j, 2 * P * (j + 1))
            codes = work.tile([P, 2 * P], U32, name="y_codes", align_bytes=64)
            nc.vector.quantize_mx(out=codes[:].bitcast(FP8X4), scales=y_plane[:, cols], in_=y_grouped[j][:])
            nc.sync.dma_start(out=y_words32[:, cols], in_=codes[:].bitcast(I32))
            if j in SCALE_STORES:
                i = SCALE_STORES.index(j)
                first = 0 if i == 0 else 2 * P * (SCALE_STORES[i - 1] + 1)
                for q in range(4):
                    nc.sync.dma_start(
                        out=y_scales32[4 * q : 4 * q + 4, first // 4 : cols.stop // 4],
                        in_=y_plane[32 * q : 32 * q + 4, first : cols.stop].bitcast(I32),
                    )

        nc.vector.memset(w_plane[:].bitcast(I32), 0)
        nc.vector.memset(len_rows[TILES : 2 * TILES, :], 0.0)
        nc.vector.memset(len_rows[2 * TILES :, :], 0.0)
        nc.vector.memset(late_rows[2 * TILES :, :], 0.0)
        nc.vector.memset(v_plane[:].bitcast(I32), 0)
        make_identity(nc, ident[:])
        nc.scalar.activation(out=ident_bf[:], in_=ident[:], func=ACT.Copy)
        load_x_tile(0)
        load_x_tile(1)
        load_x_pair(1)
        load_w(0)
        load_plane(w_plane, w_scales32)
        nc.sync.dma_start(out=len_rows[:TILES, :], in_=len_scale.rearrange("g (n p) -> (g n) p", p=P))
        load_x_pair(2)
        load_x_pair(3)
        nc.sync.dma_start(out=late_rows[:TILES, :], in_=shift.rearrange("g (n p) -> (g n) p", p=P))
        nc.sync.dma_start(out=late_rows[48:64, :], in_=cos_gain.rearrange("g (s p) -> (g s) p", p=P))
        nc.sync.dma_start(out=late_rows[32:48, :], in_=sine_term.rearrange("g (s p) -> (g s) p", p=P))
        load_v(0)
        load_plane(v_plane, v_scales32)

        def per_pair(stage, j):
            if 0 <= j < PAIRS:
                stage(j)

        def both_tiles(stage, j):
            if 0 <= j < PAIRS:
                stage(2 * j)
                stage(2 * j + 1)

        for k in range(PAIRS + 7):
            per_pair(load_x_pair, k + X_LEAD)
            u_next, phase = divmod(k + PAIRS_PER_DOMAIN, PAIRS_PER_DOMAIN)
            if u_next < G and phase == 2:
                load_w(u_next)
            if u_next < G and phase == 3:
                load_v(u_next)

            both_tiles(scale_embedding, k - 2)

            both_tiles(turn_z, k - 5)
            both_tiles(turn_x, k)
            per_pair(turn_e, k - 2)
            per_pair(turn_y, k - 6)

            per_pair(quantize_x, k - 1)
            both_tiles(exponentiate, k - 5)
            per_pair(quantize_e, k - 3)
            per_pair(quantize_y, k - 7)
            if 1 <= k < PAIRS - 1 and k % SORT_EVERY == 0:
                sort_x(2 * k + 3)
            both_tiles(margin_logits, k - 4)
            per_pair(round_y, k - 5)
            both_tiles(group_x, k)
            if k == 1:
                turn_len_scale()
            if k == 2:
                turn_late_vectors()
            per_pair(group_y, k - 6)
            per_pair(group_e, k - 2)
            if SORT_X_FROM <= k + 1 < SORT_X_UNTIL:
                sort_x(2 * k + 2)

            both_tiles(embed, k - 1)
            both_tiles(similarities, k - 3)
